import numpy as np
import ml_dtypes


def mxq(x, axis, fmt="e4m3"):
    dtype, down = {"e4m3": (ml_dtypes.float8_e4m3fn, 7), "e5m2": (ml_dtypes.float8_e5m2, 14)}[fmt]
    v = np.moveaxis(np.asarray(x, np.float32).astype(ml_dtypes.bfloat16).astype(np.float64), axis, -1)
    blocks = v.reshape(v.shape[:-1] + (-1, 32))
    amax = np.abs(blocks).max(-1, keepdims=True)
    byte = np.maximum(np.where(amax > 0, np.frexp(amax)[1] - 1 + 127, 0) - down, 1)
    scale = np.exp2(byte - 127.0)
    codes = (blocks / scale).astype(np.float32).astype(dtype).astype(np.float64)
    return np.moveaxis((codes * scale).reshape(v.shape), -1, axis)


WIDE = False


def mx_kscale(k):
    if not WIDE:
        return np.ones(k)
    levels = np.array([10, -10, 5, -5, 0])
    if k % 512:
        return np.exp2(np.random.permutation(np.resize(levels, k // 32))).repeat(32)
    a = np.empty((k // 512, 16))
    for p in range(k // 512):
        a[p, :8] = np.random.permutation(np.resize(levels, 8))
        for g in range(8):
            far = levels[np.abs(levels - a[p, g]) >= 10]
            a[p, g + 8] = far[np.random.randint(len(far))]
    return np.exp2(a.ravel()).repeat(32)


def f64(x):
    return np.asarray(x).astype(np.float64)


def striped(idx):
    return np.tile(np.asarray(idx).reshape(-1, 16).T, (8, 1)).astype(np.uint16)


def unstriped(offs):
    return offs[:16].T.reshape(-1).astype(np.int64)


E2M1 = np.array([0.0, 0.5, 1.0, 1.5, 2.0, 3.0, 4.0, 6.0, -0.0, -0.5, -1.0, -1.5, -2.0, -3.0, -4.0, -6.0])


def pack_weight(w, fmt):
    k, n = w.shape
    w = f64(np.asarray(w, np.float32).astype(ml_dtypes.bfloat16)).reshape(k // 32, 32, n)
    amax = np.abs(w).max(1)
    if fmt == "e4m3":
        byte = np.frexp(amax)[1] - 1 + 127 - 7
    else:
        mant, ex = np.frexp(amax / 6.0)
        byte = np.where(mant > 0.5, ex, ex - 1) + 127
    byte = np.clip(np.where(amax > 0, byte, 1), 1, 254)
    scaled = (w * np.exp2(127.0 - byte)[:, None, :]).reshape(k, n).astype(np.float32)
    by_word = np.ascontiguousarray(scaled.reshape(k // 512, 128, 4, n).transpose(0, 1, 3, 2))
    if fmt == "e4m3":
        words = by_word.astype(ml_dtypes.float8_e4m3fn).view(np.uint8)
    else:
        c = by_word.astype(ml_dtypes.float4_e2m1fn).view(np.uint8) & 0xF
        words = (c[..., 0::2] | (c[..., 1::2] << 4)).reshape(k // 512, 128, 2 * n)
    return np.ascontiguousarray(words), np.ascontiguousarray(byte.astype(np.uint8).reshape(k // 512, 16, n))


def unpack_weight(words, scales, fmt):
    g, _, n = scales.shape
    words = np.ascontiguousarray(words).reshape(g, 128, n, -1)
    if fmt == "e4m3":
        vals = words.view(ml_dtypes.float8_e4m3fn).astype(np.float64)
    else:
        nib = np.empty((g, 128, n, 4), np.uint8)
        nib[..., 0::2] = words & 0xF
        nib[..., 1::2] = words >> 4
        vals = E2M1[nib]
    vals = vals * np.repeat(np.exp2(scales.astype(np.float64) - 127.0), 8, axis=1)[..., None]
    return vals.transpose(0, 1, 3, 2).reshape(g * 512, n)


K, T, J, N = 512, 1024, 512, 512


def setup_inputs():
    n = np.random.standard_normal
    idx = np.random.permutation(T)[:J]
    idx2 = np.random.permutation(T)[:J]
    fk = mx_kscale(K)
    wap = pack_weight(n((K, N)) * 1 / np.sqrt(K) * fk[:, None], "e2m1")
    return {
        "xf": (n((K, T)) / fk[:, None]).astype(np.float32),
        "wa_words": wap[0],
        "wa_scales": wap[1],
        "ga": (np.random.uniform(0.4, 1.2, (1, J))).astype(np.float32),
        "old": (1.0 * n((N, T))).astype(np.float32),
        "offs": striped(idx),
        "offs2": striped(idx2),
    }


def reference(xf, wa_words, wa_scales, ga, old, offs, offs2):
    idx = unstriped(offs)
    idx2 = unstriped(offs2)
    wau = unpack_weight(wa_words, wa_scales, "e2m1")
    d = f64(xf)[:, idx] - f64(xf)[:, idx2]
    dq = mxq(d, 0, "e4m3")
    p = wau.T @ dq
    pw = p * f64(ga)
    pp = np.zeros((N, T))
    pp[:, idx2] = pw
    y = 0.5 * f64(old) - pp
    return y

@@ -1,0 +1,189 @@
+from contextlib import ExitStack
+
+import concourse.mybir as mybir
+from concourse.masks import make_identity
+
+K, T, J, N = 512, 1024, 512, 512
+FLOPS = 2 * K * J * N
+
+F32 = mybir.dt.float32
+BF16 = mybir.dt.bfloat16
+I32 = mybir.dt.int32
+U32 = mybir.dt.uint32
+U16 = mybir.dt.uint16
+U8 = mybir.dt.uint8
+FP8X4 = mybir.dt.float8_e4m3fn_x4
+FP4X4 = mybir.dt.float4_e2m1fn_x4
+MULT = mybir.AluOpType.mult
+SUB = mybir.AluOpType.subtract
+COPY = mybir.ActivationFunctionType.Copy
+
+P = 128
+PACK = 4
+BLOCKS = N // P
+BANK = 512
+HEAD = 128
+REST = J - HEAD
+MID = 256
+
+
+def tile_moe_expert_on_gap_writes_to_partner_kernel(tc, xf, wa_words, wa_scales, ga, old, offs, offs2, out):
+    nc = tc.nc
+    with ExitStack() as ctx:
+        keep = ctx.enter_context(tc.tile_pool(name="keep", bufs=1))
+        psum = ctx.enter_context(tc.psum_pool(name="psum", bufs=1))
+
+        def bank(b):
+            return psum.tile([P, BANK], F32, name="bank%d" % b)
+
+        def entries(lst, a, b):
+            return lst[:, a // 16 : b // 16]
+
+        tokens = keep.tile([P, J // 16], U16, name="tokens")
+        partners = keep.tile([P, J // 16], U16, name="partners")
+        x = [keep.tile([P, T], F32, name="x%d" % t) for t in range(PACK)]
+        x_rows = xf.rearrange("(p t) c -> p t c", t=PACK)
+        nc.sync.dma_start(x[0][:], x_rows[:, 0, :])
+        nc.sync.dma_start(partners[:], offs2)
+        nc.sync.dma_start(tokens[:], offs)
+        for t in range(1, PACK):
+            nc.sync.dma_start(x[t][:], x_rows[:, t, :])
+        ga_cols = keep.tile([P, PACK], F32, name="ga_cols")
+        nc.sync.dma_start(ga_cols[:], ga.rearrange("o (p c) -> (o p) c", c=PACK))
+        w_words = keep.tile([P, 2 * N], U8, name="w_words", align_bytes=64)
+        nc.sync.dma_start(w_words[:].bitcast(I32), wa_words[0].bitcast(I32))
+        w_scales = keep.tile([P, N], U8, name="w_scales", align_bytes=64)
+        nc.gpsimd.memset(w_scales[:].bitcast(I32), 0)
+        for q in range(4):
+            nc.sync.dma_start(w_scales[32 * q : 32 * q + 4, :].bitcast(I32), wa_scales[0, 4 * q : 4 * q + 4, :].bitcast(I32))
+        state = [keep.tile([P, T], F32, name="state%d" % b) for b in range(BLOCKS)]
+        for b in range(BLOCKS):
+            nc.sync.dma_start(state[b][:], old[b * P : (b + 1) * P, :])
+
+        ident = keep.tile([P, P], F32, name="ident")
+        make_identity(nc, ident[:])
+        placed = [keep.tile([P, T], F32, name="placed%d" % b) for b in range(BLOCKS)]
+        for b in range(BLOCKS):
+            nc.vector.memset(placed[b][:], 0.0)
+
+        spread = bank(7)
+        for c in range(PACK):
+            nc.tensor.transpose(spread[:, c * P : (c + 1) * P], ga_cols[:, c : c + 1].to_broadcast([P, P]), ident[:])
+        gate = keep.tile([P, J], F32, name="gate")
+        gate_twice = keep.tile([P, J], F32, name="gate_twice")
+        spread_j = spread[:].rearrange("m (c p) -> m p c", c=PACK)
+        nc.scalar.activation(gate_twice[:].rearrange("m (p c) -> m p c", c=PACK), spread_j, COPY, scale=-2.0)
+        nc.scalar.copy(gate[:].rearrange("m (p c) -> m p c", c=PACK), spread_j)
+
+        work = keep.tile([P, PACK * REST], F32, name="work")
+        d_rest = work[:].rearrange("p (t c) -> p t c", t=PACK)
+        d_head = work[:, REST : REST + 8 * HEAD].rearrange("p (t c) -> p t c", t=PACK)[:, :, 0:HEAD]
+        g_head = keep.tile([P, PACK - 1, HEAD], F32, name="g_head")
+        g_rest = keep.tile([P, PACK, REST], F32, name="g_rest")
+        for t in range(PACK):
+            last = t == PACK - 1
+            gh = work[:, 0:HEAD] if last else g_head[:, t, :]
+            cut = HEAD if last else REST
+            nc.vector.tensor_copy(gh, x[t][:].indirect(entries(partners, 0, HEAD)))
+            nc.vector.tensor_copy(g_rest[:, t, 0:cut], x[t][:].indirect(entries(partners, HEAD, HEAD + cut)))
+            nc.vector.tensor_tensor(d_head[:, t, :], x[t][:].indirect(entries(tokens, 0, HEAD)), gh, SUB)
+            if last:
+                nc.vector.tensor_copy(g_rest[:, t, cut:REST], x[t][:].indirect(entries(partners, HEAD + cut, J)))
+
+        grouped = keep.tile([P, PACK * J], BF16, name="grouped", align_bytes=64)
+        codes = keep.tile([P, J], U32, name="codes", align_bytes=64)
+        scales = keep.tile([P, J], U8, name="scales", align_bytes=64)
+
+        def interleave(a, b, planes):
+            nc.scalar.copy(
+                grouped[:, PACK * a : PACK * b].rearrange("p (c i t) -> p c t i", i=4, t=PACK),
+                planes.rearrange("p t (c i) -> p c t i", i=4),
+            )
+
+        def quantize(a, b):
+            nc.vector.quantize_mx(out=codes[:, a:b].bitcast(FP8X4), scales=scales[:, a:b], in_=grouped[:, PACK * a : PACK * b])
+
+        def multiply(acc, blk, a, b):
+            nc.tensor.matmul_mx(
+                out=acc,
+                lhsT=w_words[:, 2 * P * blk : 2 * P * (blk + 1)].bitcast(FP4X4),
+                lhsT_scale=w_scales[:, P * blk : P * (blk + 1)],
+                rhs=codes[:, a:b].bitcast(FP8X4),
+                rhs_scale=scales[:, a:b],
+                start=True,
+                stop=True,
+            )
+
+        def gap_rest(t):
+            nc.vector.tensor_tensor(d_rest[:, t, :], x[t][:].indirect(entries(tokens, HEAD, J)), g_rest[:, t, :], SUB)
+
+        def scatter(blk, a, b, src):
+            g = gate if blk == BLOCKS - 1 else gate_twice
+            nc.vector.tensor_tensor(placed[blk][:].indirect(entries(partners, a, b)), src, g[:, a:b], MULT)
+
+        interleave(0, HEAD, d_head)
+        gap_rest(0)
+        quantize(0, HEAD)
+        acc_head = bank(0)
+        for blk in range(BLOCKS):
+            multiply(acc_head[:, blk * HEAD : (blk + 1) * HEAD], blk, 0, HEAD)
+        p_head = keep.tile([P, 2, HEAD], F32, name="p_head")
+        nc.scalar.copy(p_head[:].rearrange("p b c -> p (b c)"), acc_head[:, 0 : 2 * HEAD])
+        for t in range(1, PACK):
+            gap_rest(t)
+
+        interleave(HEAD, HEAD + MID, d_rest[:, :, 0:MID])
+        scatter(0, 0, HEAD, p_head[:, 0, :])
+        scatter(1, 0, HEAD, p_head[:, 1, :])
+        quantize(HEAD, HEAD + MID)
+        acc_rest = [bank(1 + blk) for blk in range(BLOCKS)]
+        for blk in range(BLOCKS):
+            multiply(acc_rest[blk][:, 0:MID], blk, HEAD, HEAD + MID)
+        nc.scalar.copy(work[:, 0:HEAD], acc_head[:, 2 * HEAD : 3 * HEAD])
+        interleave(HEAD + MID, J, d_rest[:, :, MID:REST])
+        scatter(2, 0, HEAD, work[:, 0:HEAD])
+        quantize(HEAD + MID, J)
+        p_rest = keep.tile([P, BLOCKS, J], F32, name="p_rest")
+        nc.scalar.copy(p_rest[:, 0, HEAD : HEAD + MID], acc_rest[0][:, 0:MID])
+        scatter(0, HEAD, HEAD + MID, p_rest[:, 0, HEAD : HEAD + MID])
+        for blk in range(BLOCKS):
+            multiply(acc_rest[blk][:, MID:REST], blk, HEAD + MID, J)
+        for blk in range(BLOCKS):
+            done = MID if blk == 0 else 0
+            nc.scalar.copy(p_rest[:, blk, HEAD + done : J], acc_rest[blk][:, done:REST])
+        nc.scalar.copy(p_rest[:, BLOCKS - 1, 0:HEAD], acc_head[:, 3 * HEAD : 4 * HEAD])
+        first = [HEAD + MID, HEAD, HEAD, 0]
+
+        sum_banks = [(5, 6), (7, 0), (5, 6)]
+        back_banks = [(1, 2), (3, 4), (1, 2)]
+        for blk in range(BLOCKS):
+            rows = slice(blk * P, (blk + 1) * P)
+            result = keep.tile([P, T], F32, name="result%d" % blk)
+            if blk == BLOCKS - 1:
+                scatter(blk, first[blk], J, p_rest[:, blk, first[blk] : J])
+                for h in range(2):
+                    cols = slice(h * BANK, (h + 1) * BANK)
+                    nc.vector.scalar_tensor_tensor(result[:, cols], state[blk][:, cols], 0.5, placed[blk][:, cols], MULT, SUB)
+                    nc.sync.dma_start(out[rows, cols], result[:, cols])
+                continue
+            sums = [bank(b) for b in sum_banks[blk]]
+            for h in range(2):
+                for c in range(4):
+                    col = h * BANK + c * P
+                    nc.tensor.matmul(sums[h][:, c * P : (c + 1) * P], state[blk][:, col : col + P], ident[:], start=(c == 0), stop=False, is_transpose=True)
+            scatter(blk, first[blk], J, p_rest[:, blk, first[blk] : J])
+            turned = keep.tile([P, T], F32, name="turned%d" % blk)
+            for h in range(2):
+                cols = slice(h * BANK, (h + 1) * BANK)
+                for c in range(4):
+                    col = h * BANK + c * P
+                    nc.tensor.matmul(sums[h][:, c * P : (c + 1) * P], placed[blk][:, col : col + P], ident[:], start=False, stop=(c == 3), is_transpose=True)
+                nc.scalar.activation(turned[:, cols], sums[h][:], COPY, scale=0.5)
+            for h in range(2):
+                cols = slice(h * BANK, (h + 1) * BANK)
+                back = bank(back_banks[blk][h])
+                for c in range(4):
+                    col = h * BANK + c * P
+                    nc.tensor.transpose(back[:, c * P : (c + 1) * P], turned[:, col : col + P], ident[:])
+                nc.scalar.copy(result[:, cols], back[:])
+                nc.sync.dma_start(out[rows, cols], result[:, cols])

@@ -64,7 +64,7 @@ def tile_moe_expert_on_gap_writes_to_partner_kernel(tc, xf, wa_words, wa_scales,
         make_identity(nc, ident[:])
         placed = [keep.tile([P, T], F32, name="placed%d" % b) for b in range(BLOCKS)]
         for b in range(BLOCKS):
-            nc.vector.memset(placed[b][:], 0.0)
+            (nc.vector if b < 2 else nc.gpsimd).memset(placed[b][:].bitcast(I32), 0)
 
         spread = bank(7)
         for c in range(PACK):
@@ -118,7 +118,7 @@ def tile_moe_expert_on_gap_writes_to_partner_kernel(tc, xf, wa_words, wa_scales,
             nc.vector.tensor_tensor(d_rest[:, t, :], x[t][:].indirect(entries(tokens, HEAD, J)), g_rest[:, t, :], SUB)
 
         def scatter(blk, a, b, src):
-            g = gate if blk == BLOCKS - 1 else gate_twice
+            g = gate if blk >= 2 else gate_twice
             nc.vector.tensor_tensor(placed[blk][:].indirect(entries(partners, a, b)), src, g[:, a:b], MULT)
 
         interleave(0, HEAD, d_head)
@@ -159,7 +159,7 @@ def tile_moe_expert_on_gap_writes_to_partner_kernel(tc, xf, wa_words, wa_scales,
         for blk in range(BLOCKS):
             rows = slice(blk * P, (blk + 1) * P)
             result = keep.tile([P, T], F32, name="result%d" % blk)
-            if blk == BLOCKS - 1:
+            if blk >= 2:
                 scatter(blk, first[blk], J, p_rest[:, blk, first[blk] : J])
                 for h in range(2):
                     cols = slice(h * BANK, (h + 1) * BANK)
@@ -186,4 +186,4 @@ def tile_moe_expert_on_gap_writes_to_partner_kernel(tc, xf, wa_words, wa_scales,
                     col = h * BANK + c * P
                     nc.tensor.transpose(back[:, c * P : (c + 1) * P], turned[:, col : col + P], ident[:])
                 nc.scalar.copy(result[:, cols], back[:])
-                nc.sync.dma_start(out[rows, cols], result[:, cols])
+                nc.scalar.dma_start(out[rows, cols], result[:, cols])

@@ -46,10 +46,12 @@ def tile_moe_expert_on_gap_writes_to_partner_kernel(tc, xf, wa_words, wa_scales,
         nc.sync.dma_start(x[0][:], x_rows[:, 0, :])
         nc.sync.dma_start(partners[:], offs2)
         nc.sync.dma_start(tokens[:], offs)
-        for t in range(1, PACK):
-            nc.sync.dma_start(x[t][:], x_rows[:, t, :])
+        nc.sync.dma_start(x[1][:], x_rows[:, 1, :])
         ga_cols = keep.tile([P, PACK], F32, name="ga_cols")
-        nc.sync.dma_start(ga_cols[:], ga.rearrange("o (p c) -> (o p) c", c=PACK))
+        with nc.allow_non_contiguous_dma(reason="one weight a slot, slots on partitions"):
+            nc.sync.dma_start(ga_cols[:], ga.rearrange("o (c p) -> p (o c)", p=P))
+        for t in range(2, PACK):
+            nc.sync.dma_start(x[t][:], x_rows[:, t, :])
         w_words = keep.tile([P, 2 * N], U8, name="w_words", align_bytes=64)
         nc.sync.dma_start(w_words[:].bitcast(I32), wa_words[0].bitcast(I32))
         w_scales = keep.tile([P, N], U8, name="w_scales", align_bytes=64)
@@ -66,14 +68,13 @@ def tile_moe_expert_on_gap_writes_to_partner_kernel(tc, xf, wa_words, wa_scales,
         for b in range(BLOCKS):
             (nc.vector if b < 2 else nc.gpsimd).memset(placed[b][:].bitcast(I32), 0)
 
-        spread = bank(7)
+        spread = bank(5)
         for c in range(PACK):
             nc.tensor.transpose(spread[:, c * P : (c + 1) * P], ga_cols[:, c : c + 1].to_broadcast([P, P]), ident[:])
         gate = keep.tile([P, J], F32, name="gate")
         gate_twice = keep.tile([P, J], F32, name="gate_twice")
-        spread_j = spread[:].rearrange("m (c p) -> m p c", c=PACK)
-        nc.scalar.activation(gate_twice[:].rearrange("m (p c) -> m p c", c=PACK), spread_j, COPY, scale=-2.0)
-        nc.scalar.copy(gate[:].rearrange("m (p c) -> m p c", c=PACK), spread_j)
+        nc.scalar.activation(gate_twice[:], spread[:], COPY, scale=-2.0)
+        nc.scalar.copy(gate[:], spread[:])
 
         work = keep.tile([P, PACK * REST], F32, name="work")
         d_rest = work[:].rearrange("p (t c) -> p t c", t=PACK)
@@ -125,7 +126,7 @@ def tile_moe_expert_on_gap_writes_to_partner_kernel(tc, xf, wa_words, wa_scales,
         gap_rest(0)
         quantize(0, HEAD)
         acc_head = bank(0)
-        for blk in range(BLOCKS):
+        for blk in range(3):
             multiply(acc_head[:, blk * HEAD : (blk + 1) * HEAD], blk, 0, HEAD)
         p_head = keep.tile([P, 2, HEAD], F32, name="p_head")
         nc.scalar.copy(p_head[:].rearrange("p b c -> p (b c)"), acc_head[:, 0 : 2 * HEAD])
@@ -136,8 +137,8 @@ def tile_moe_expert_on_gap_writes_to_partner_kernel(tc, xf, wa_words, wa_scales,
         scatter(0, 0, HEAD, p_head[:, 0, :])
         scatter(1, 0, HEAD, p_head[:, 1, :])
         quantize(HEAD, HEAD + MID)
-        acc_rest = [bank(1 + blk) for blk in range(BLOCKS)]
-        for blk in range(BLOCKS):
+        acc_rest = [bank(1 + blk) for blk in range(3)]
+        for blk in range(3):
             multiply(acc_rest[blk][:, 0:MID], blk, HEAD, HEAD + MID)
         nc.scalar.copy(work[:, 0:HEAD], acc_head[:, 2 * HEAD : 3 * HEAD])
         interleave(HEAD + MID, J, d_rest[:, :, MID:REST])
@@ -146,21 +147,51 @@ def tile_moe_expert_on_gap_writes_to_partner_kernel(tc, xf, wa_words, wa_scales,
         p_rest = keep.tile([P, BLOCKS, J], F32, name="p_rest")
         nc.scalar.copy(p_rest[:, 0, HEAD : HEAD + MID], acc_rest[0][:, 0:MID])
         scatter(0, HEAD, HEAD + MID, p_rest[:, 0, HEAD : HEAD + MID])
-        for blk in range(BLOCKS):
+        multiply(acc_head[:, 3 * HEAD : 4 * HEAD], 0, HEAD + MID, J)
+        for blk in (1, 2):
             multiply(acc_rest[blk][:, MID:REST], blk, HEAD + MID, J)
-        for blk in range(BLOCKS):
-            done = MID if blk == 0 else 0
-            nc.scalar.copy(p_rest[:, blk, HEAD + done : J], acc_rest[blk][:, done:REST])
-        nc.scalar.copy(p_rest[:, BLOCKS - 1, 0:HEAD], acc_head[:, 3 * HEAD : 4 * HEAD])
+        nc.scalar.copy(p_rest[:, 0, HEAD + MID : J], acc_head[:, 3 * HEAD : 4 * HEAD])
+        for blk in (1, 2):
+            nc.scalar.copy(p_rest[:, blk, HEAD:J], acc_rest[blk][:, 0:REST])
         first = [HEAD + MID, HEAD, HEAD, 0]
 
-        sum_banks = [(5, 6), (7, 0), (5, 6)]
-        back_banks = [(1, 2), (3, 4), (1, 2)]
+        by_slot = bank(4)
+        weighted = keep.tile([P, J], F32, name="weighted")
+        for c in range(4):
+            nc.tensor.matmul_mx(
+                out=by_slot[:, c * P : (c + 1) * P],
+                lhsT=codes[:, c * P : (c + 1) * P].bitcast(FP8X4),
+                lhsT_scale=scales[:, c * P : (c + 1) * P],
+                rhs=w_words[:, 2 * P * 3 : 2 * P * 4].bitcast(FP4X4),
+                rhs_scale=w_scales[:, P * 3 : P * 4],
+                start=True,
+                stop=True,
+            )
+        for c in range(4):
+            nc.scalar.activation(weighted[:, c * P : (c + 1) * P], by_slot[:, c * P : (c + 1) * P], COPY, scale=ga_cols[:, c : c + 1])
+        by_row = bank(1)
+        for c in range(4):
+            nc.tensor.transpose(by_row[:, c * P : (c + 1) * P], weighted[:, c * P : (c + 1) * P], ident[:])
+        nc.scalar.copy(p_rest[:, 3, :], by_row[:])
+        half_state = work[:, BANK : BANK + T]
+        for h in range(2):
+            cols = slice(h * BANK, (h + 1) * BANK)
+            nc.scalar.activation(half_state[:, cols], state[2][:, cols], COPY, scale=0.5)
+
+        sum_banks = [(6, 7), (5, 0)]
+        back_banks = [(2, 3), (4, 1)]
         for blk in range(BLOCKS):
             rows = slice(blk * P, (blk + 1) * P)
             result = keep.tile([P, T], F32, name="result%d" % blk)
-            if blk >= 2:
+            if blk == 2:
                 scatter(blk, first[blk], J, p_rest[:, blk, first[blk] : J])
+                for h in range(2):
+                    cols = slice(h * BANK, (h + 1) * BANK)
+                    nc.gpsimd.tensor_tensor(result[:, cols], half_state[:, cols], placed[blk][:, cols], SUB)
+                    nc.sync.dma_start(out[rows, cols], result[:, cols])
+                continue
+            if blk == 3:
+                nc.vector.tensor_copy(placed[blk][:].indirect(partners[:]), p_rest[:, blk, :])
                 for h in range(2):
                     cols = slice(h * BANK, (h + 1) * BANK)
                     nc.vector.scalar_tensor_tensor(result[:, cols], state[blk][:, cols], 0.5, placed[blk][:, cols], MULT, SUB)

@@ -22,9 +22,8 @@ P = 128
 PACK = 4
 BLOCKS = N // P
 BANK = 512
-HEAD = 128
+HEAD = 256
 REST = J - HEAD
-MID = 256
 
 
 def tile_moe_expert_on_gap_writes_to_partner_kernel(tc, xf, wa_words, wa_scales, ga, old, offs, offs2, out):
@@ -45,8 +44,8 @@ def tile_moe_expert_on_gap_writes_to_partner_kernel(tc, xf, wa_words, wa_scales,
         x_rows = xf.rearrange("(p t) c -> p t c", t=PACK)
         nc.sync.dma_start(x[0][:], x_rows[:, 0, :])
         nc.sync.dma_start(partners[:], offs2)
-        nc.sync.dma_start(tokens[:], offs)
         nc.sync.dma_start(x[1][:], x_rows[:, 1, :])
+        nc.sync.dma_start(tokens[:], offs)
         ga_cols = keep.tile([P, PACK], F32, name="ga_cols")
         with nc.allow_non_contiguous_dma(reason="one weight a slot, slots on partitions"):
             nc.sync.dma_start(ga_cols[:], ga.rearrange("o (c p) -> p (o c)", p=P))
@@ -59,14 +58,14 @@ def tile_moe_expert_on_gap_writes_to_partner_kernel(tc, xf, wa_words, wa_scales,
         for q in range(4):
             nc.sync.dma_start(w_scales[32 * q : 32 * q + 4, :].bitcast(I32), wa_scales[0, 4 * q : 4 * q + 4, :].bitcast(I32))
         state = [keep.tile([P, T], F32, name="state%d" % b) for b in range(BLOCKS)]
-        for b in range(BLOCKS):
+        for b in (1, 0, 2, 3):
             nc.sync.dma_start(state[b][:], old[b * P : (b + 1) * P, :])
 
         ident = keep.tile([P, P], F32, name="ident")
         make_identity(nc, ident[:])
         placed = [keep.tile([P, T], F32, name="placed%d" % b) for b in range(BLOCKS)]
         for b in range(BLOCKS):
-            (nc.vector if b < 2 else nc.gpsimd).memset(placed[b][:].bitcast(I32), 0)
+            nc.gpsimd.memset(placed[b][:].bitcast(I32), 0)
 
         spread = bank(5)
         for c in range(PACK):
@@ -76,20 +75,29 @@ def tile_moe_expert_on_gap_writes_to_partner_kernel(tc, xf, wa_words, wa_scales,
         nc.scalar.activation(gate_twice[:], spread[:], COPY, scale=-2.0)
         nc.scalar.copy(gate[:], spread[:])
 
-        work = keep.tile([P, PACK * REST], F32, name="work")
-        d_rest = work[:].rearrange("p (t c) -> p t c", t=PACK)
-        d_head = work[:, REST : REST + 8 * HEAD].rearrange("p (t c) -> p t c", t=PACK)[:, :, 0:HEAD]
-        g_head = keep.tile([P, PACK - 1, HEAD], F32, name="g_head")
-        g_rest = keep.tile([P, PACK, REST], F32, name="g_rest")
-        for t in range(PACK):
-            last = t == PACK - 1
-            gh = work[:, 0:HEAD] if last else g_head[:, t, :]
-            cut = HEAD if last else REST
-            nc.vector.tensor_copy(gh, x[t][:].indirect(entries(partners, 0, HEAD)))
-            nc.vector.tensor_copy(g_rest[:, t, 0:cut], x[t][:].indirect(entries(partners, HEAD, HEAD + cut)))
-            nc.vector.tensor_tensor(d_head[:, t, :], x[t][:].indirect(entries(tokens, 0, HEAD)), gh, SUB)
-            if last:
-                nc.vector.tensor_copy(g_rest[:, t, cut:REST], x[t][:].indirect(entries(partners, HEAD + cut, J)))
+        work = keep.tile([P, 6 * HEAD], F32, name="work")
+        d_rest = work[:, 0 : PACK * REST].rearrange("p (t c) -> p t c", t=PACK)
+        d_head = work[:, 2 * HEAD : 6 * HEAD].rearrange("p (t c) -> p t c", t=PACK)
+        g = keep.tile([P, PACK, J], F32, name="g")
+        g_last = work[:, HEAD // 2 : 3 * HEAD // 2]
+
+        def fetch(dst, t, a, b):
+            nc.vector.tensor_copy(dst, x[t][:].indirect(entries(partners, a, b)))
+
+        def gap_head(t, src):
+            nc.vector.tensor_tensor(d_head[:, t, :], x[t][:].indirect(entries(tokens, 0, HEAD)), src, SUB)
+
+        fetch(g[:, 0, :], 0, 0, J)
+        fetch(g[:, 1, :], 1, 0, J)
+        gap_head(0, g[:, 0, 0:HEAD])
+        gap_head(1, g[:, 1, 0:HEAD])
+        fetch(g[:, 2, 0:HEAD], 2, 0, HEAD)
+        fetch(g[:, 2, HEAD:J], 2, HEAD, J)
+        gap_head(2, g[:, 2, 0:HEAD])
+        fetch(g_last, 3, 0, HEAD)
+        fetch(g[:, 3, HEAD : HEAD + P], 3, HEAD, HEAD + P)
+        gap_head(3, g_last)
+        fetch(g[:, 3, HEAD + P : J], 3, HEAD + P, J)
 
         grouped = keep.tile([P, PACK * J], BF16, name="grouped", align_bytes=64)
         codes = keep.tile([P, J], U32, name="codes", align_bytes=64)
@@ -116,105 +124,116 @@ def tile_moe_expert_on_gap_writes_to_partner_kernel(tc, xf, wa_words, wa_scales,
             )
 
         def gap_rest(t):
-            nc.vector.tensor_tensor(d_rest[:, t, :], x[t][:].indirect(entries(tokens, HEAD, J)), g_rest[:, t, :], SUB)
+            nc.vector.tensor_tensor(d_rest[:, t, :], x[t][:].indirect(entries(tokens, HEAD, J)), g[:, t, HEAD:J], SUB)
 
         def scatter(blk, a, b, src):
-            g = gate if blk >= 2 else gate_twice
-            nc.vector.tensor_tensor(placed[blk][:].indirect(entries(partners, a, b)), src, g[:, a:b], MULT)
+            factor = gate if blk == 1 else gate_twice
+            nc.vector.tensor_tensor(placed[blk][:].indirect(entries(partners, a, b)), src, factor[:, a:b], MULT)
 
-        interleave(0, HEAD, d_head)
-        gap_rest(0)
-        quantize(0, HEAD)
-        acc_head = bank(0)
-        for blk in range(3):
-            multiply(acc_head[:, blk * HEAD : (blk + 1) * HEAD], blk, 0, HEAD)
-        p_head = keep.tile([P, 2, HEAD], F32, name="p_head")
-        nc.scalar.copy(p_head[:].rearrange("p b c -> p (b c)"), acc_head[:, 0 : 2 * HEAD])
-        for t in range(1, PACK):
-            gap_rest(t)
+        by_slot = [bank(3), bank(4)]
+        weighted = keep.tile([P, 4, 2 * P], F32, name="weighted")
+        by_row2 = bank(5)
 
-        interleave(HEAD, HEAD + MID, d_rest[:, :, 0:MID])
-        scatter(0, 0, HEAD, p_head[:, 0, :])
-        scatter(1, 0, HEAD, p_head[:, 1, :])
-        quantize(HEAD, HEAD + MID)
-        acc_rest = [bank(1 + blk) for blk in range(3)]
-        for blk in range(3):
-            multiply(acc_rest[blk][:, 0:MID], blk, HEAD, HEAD + MID)
-        nc.scalar.copy(work[:, 0:HEAD], acc_head[:, 2 * HEAD : 3 * HEAD])
-        interleave(HEAD + MID, J, d_rest[:, :, MID:REST])
-        scatter(2, 0, HEAD, work[:, 0:HEAD])
-        quantize(HEAD + MID, J)
-        p_rest = keep.tile([P, BLOCKS, J], F32, name="p_rest")
-        nc.scalar.copy(p_rest[:, 0, HEAD : HEAD + MID], acc_rest[0][:, 0:MID])
-        scatter(0, HEAD, HEAD + MID, p_rest[:, 0, HEAD : HEAD + MID])
-        multiply(acc_head[:, 3 * HEAD : 4 * HEAD], 0, HEAD + MID, J)
-        for blk in (1, 2):
-            multiply(acc_rest[blk][:, MID:REST], blk, HEAD + MID, J)
-        nc.scalar.copy(p_rest[:, 0, HEAD + MID : J], acc_head[:, 3 * HEAD : 4 * HEAD])
-        for blk in (1, 2):
-            nc.scalar.copy(p_rest[:, blk, HEAD:J], acc_rest[blk][:, 0:REST])
-        first = [HEAD + MID, HEAD, HEAD, 0]
-
-        by_slot = bank(4)
-        weighted = keep.tile([P, J], F32, name="weighted")
-        for c in range(4):
+        def slots_first(c):
             nc.tensor.matmul_mx(
-                out=by_slot[:, c * P : (c + 1) * P],
+                out=by_slot[c // 2][:, (c % 2) * 2 * P : (c % 2 + 1) * 2 * P],
                 lhsT=codes[:, c * P : (c + 1) * P].bitcast(FP8X4),
                 lhsT_scale=scales[:, c * P : (c + 1) * P],
-                rhs=w_words[:, 2 * P * 3 : 2 * P * 4].bitcast(FP4X4),
-                rhs_scale=w_scales[:, P * 3 : P * 4],
+                rhs=w_words[:, 2 * P * 2 : 2 * P * 4].bitcast(FP4X4),
+                rhs_scale=w_scales[:, P * 2 : P * 4],
                 start=True,
                 stop=True,
             )
+
+        def weigh(c):
+            nc.scalar.activation(weighted[:, c, :], by_slot[c // 2][:, (c % 2) * 2 * P : (c % 2 + 1) * 2 * P], COPY, scale=ga_cols[:, c : c + 1])
+
+        def turn(dst, blk, c):
+            nc.tensor.transpose(dst[:, c * P : (c + 1) * P], weighted[:, c, (blk - 2) * P : (blk - 1) * P], ident[:])
+
+        def place(blk, a, b, src):
+            nc.vector.tensor_copy(placed[blk][:].indirect(entries(partners, a, b)), src)
+
+        def halve(dst, blk):
+            for h in range(2):
+                cols = slice(h * BANK, (h + 1) * BANK)
+                nc.scalar.activation(dst[:, cols], state[blk][:, cols], COPY, scale=0.5)
+
+        interleave(0, HEAD, d_head)
+        gap_rest(0)
+        gap_rest(1)
+        quantize(0, HEAD)
+        acc_head = bank(0)
+        for blk in range(2):
+            multiply(acc_head[:, blk * HEAD : (blk + 1) * HEAD], blk, 0, HEAD)
+        slots_first(0)
+        slots_first(1)
+        p_head = keep.tile([P, HEAD], F32, name="p_head")
+        nc.scalar.copy(p_head[:], acc_head[:, 0:HEAD])
+        gap_rest(2)
+        gap_rest(3)
+
+        interleave(HEAD, J, d_rest)
+        scatter(0, 0, HEAD, p_head[:])
+        quantize(HEAD, J)
+        acc_rest = bank(1)
+        for blk in range(2):
+            multiply(acc_rest[:, blk * REST : (blk + 1) * REST], blk, HEAD, J)
+        slots_first(2)
+        slots_first(3)
+        nc.scalar.copy(work[:, 0:HEAD], acc_head[:, HEAD : 2 * HEAD])
+        scatter(1, 0, HEAD, work[:, 0:HEAD])
+        p_rest = keep.tile([P, BLOCKS, J], F32, name="p_rest")
+        for blk in range(2):
+            nc.scalar.copy(p_rest[:, blk, HEAD:J], acc_rest[:, blk * REST : (blk + 1) * REST])
         for c in range(4):
-            nc.scalar.activation(weighted[:, c * P : (c + 1) * P], by_slot[:, c * P : (c + 1) * P], COPY, scale=ga_cols[:, c : c + 1])
-        by_row = bank(1)
+            weigh(c)
+        by_row3 = bank(2)
         for c in range(4):
-            nc.tensor.transpose(by_row[:, c * P : (c + 1) * P], weighted[:, c * P : (c + 1) * P], ident[:])
-        nc.scalar.copy(p_rest[:, 3, :], by_row[:])
-        half_state = work[:, BANK : BANK + T]
+            turn(by_row2, 2, c)
+        for c in range(4):
+            turn(by_row3, 3, c)
+        nc.scalar.copy(p_rest[:, 2, :], by_row2[:])
+        nc.scalar.copy(p_rest[:, 3, :], by_row3[:])
+        half1 = keep.tile([P, T], F32, name="half1")
+        halve(half1, 1)
+        half2 = work[:, BANK : BANK + T]
+        halve(half2, 2)
+        result = [keep.tile([P, T], F32, name="result%d" % b) for b in range(BLOCKS)]
+
+        def on_gpsimd(blk, half):
+            for h in range(2):
+                cols = slice(h * BANK, (h + 1) * BANK)
+                nc.gpsimd.tensor_tensor(result[blk][:, cols], half[:, cols], placed[blk][:, cols], SUB)
+                nc.sync.dma_start(out[blk * P : (blk + 1) * P, cols], result[blk][:, cols])
+
+        sums = [bank(5), bank(2)]
+        for h in range(2):
+            for c in range(4):
+                col = h * BANK + c * P
+                nc.tensor.matmul(sums[h][:, c * P : (c + 1) * P], state[0][:, col : col + P], ident[:], start=(c == 0), stop=False, is_transpose=True)
+        scatter(0, HEAD, J, p_rest[:, 0, HEAD:J])
+        turned = keep.tile([P, T], F32, name="turned")
         for h in range(2):
             cols = slice(h * BANK, (h + 1) * BANK)
-            nc.scalar.activation(half_state[:, cols], state[2][:, cols], COPY, scale=0.5)
+            for c in range(4):
+                col = h * BANK + c * P
+                nc.tensor.matmul(sums[h][:, c * P : (c + 1) * P], placed[0][:, col : col + P], ident[:], start=False, stop=(c == 3), is_transpose=True)
+            nc.scalar.activation(turned[:, cols], sums[h][:], COPY, scale=0.5)
+        for h in range(2):
+            cols = slice(h * BANK, (h + 1) * BANK)
+            back = bank(3 + h)
+            for c in range(4):
+                col = h * BANK + c * P
+                nc.tensor.transpose(back[:, c * P : (c + 1) * P], turned[:, col : col + P], ident[:])
+            nc.scalar.copy(result[0][:, cols], back[:])
+            nc.scalar.dma_start(out[0:P, cols], result[0][:, cols])
 
-        sum_banks = [(6, 7), (5, 0)]
-        back_banks = [(2, 3), (4, 1)]
-        for blk in range(BLOCKS):
-            rows = slice(blk * P, (blk + 1) * P)
-            result = keep.tile([P, T], F32, name="result%d" % blk)
-            if blk == 2:
-                scatter(blk, first[blk], J, p_rest[:, blk, first[blk] : J])
-                for h in range(2):
-                    cols = slice(h * BANK, (h + 1) * BANK)
-                    nc.gpsimd.tensor_tensor(result[:, cols], half_state[:, cols], placed[blk][:, cols], SUB)
-                    nc.sync.dma_start(out[rows, cols], result[:, cols])
-                continue
-            if blk == 3:
-                nc.vector.tensor_copy(placed[blk][:].indirect(partners[:]), p_rest[:, blk, :])
-                for h in range(2):
-                    cols = slice(h * BANK, (h + 1) * BANK)
-                    nc.vector.scalar_tensor_tensor(result[:, cols], state[blk][:, cols], 0.5, placed[blk][:, cols], MULT, SUB)
-                    nc.sync.dma_start(out[rows, cols], result[:, cols])
-                continue
-            sums = [bank(b) for b in sum_banks[blk]]
-            for h in range(2):
-                for c in range(4):
-                    col = h * BANK + c * P
-                    nc.tensor.matmul(sums[h][:, c * P : (c + 1) * P], state[blk][:, col : col + P], ident[:], start=(c == 0), stop=False, is_transpose=True)
-            scatter(blk, first[blk], J, p_rest[:, blk, first[blk] : J])
-            turned = keep.tile([P, T], F32, name="turned%d" % blk)
-            for h in range(2):
-                cols = slice(h * BANK, (h + 1) * BANK)
-                for c in range(4):
-                    col = h * BANK + c * P
-                    nc.tensor.matmul(sums[h][:, c * P : (c + 1) * P], placed[blk][:, col : col + P], ident[:], start=False, stop=(c == 3), is_transpose=True)
-                nc.scalar.activation(turned[:, cols], sums[h][:], COPY, scale=0.5)
-            for h in range(2):
-                cols = slice(h * BANK, (h + 1) * BANK)
-                back = bank(back_banks[blk][h])
-                for c in range(4):
-                    col = h * BANK + c * P
-                    nc.tensor.transpose(back[:, c * P : (c + 1) * P], turned[:, col : col + P], ident[:])
-                nc.scalar.copy(result[:, cols], back[:])
-                nc.scalar.dma_start(out[rows, cols], result[:, cols])
+        scatter(1, HEAD, J, p_rest[:, 1, HEAD:J])
+        on_gpsimd(1, half1)
+        place(2, 0, J, p_rest[:, 2, :])
+        on_gpsimd(2, half2)
+        place(3, 0, J, p_rest[:, 3, :])
+        for cols in (slice(0, 320), slice(320, 672), slice(672, T)):
+            nc.vector.scalar_tensor_tensor(result[3][:, cols], state[3][:, cols], 0.5, placed[3][:, cols], MULT, SUB)
+            nc.sync.dma_start(out[3 * P : 4 * P, cols], result[3][:, cols])

from contextlib import ExitStack

import concourse.mybir as mybir
from concourse.masks import make_identity

K, T, J, N = 512, 1024, 512, 512
FLOPS = 2 * K * J * N

F32 = mybir.dt.float32
BF16 = mybir.dt.bfloat16
I32 = mybir.dt.int32
U32 = mybir.dt.uint32
U16 = mybir.dt.uint16
U8 = mybir.dt.uint8
FP8X4 = mybir.dt.float8_e4m3fn_x4
FP4X4 = mybir.dt.float4_e2m1fn_x4
MULT = mybir.AluOpType.mult
SUB = mybir.AluOpType.subtract
COPY = mybir.ActivationFunctionType.Copy

P = 128
PACK = 4
BLOCKS = N // P
BANK = 512
HEAD = 256
REST = J - HEAD


def tile_moe_expert_on_gap_writes_to_partner_kernel(tc, xf, wa_words, wa_scales, ga, old, offs, offs2, out):
    nc = tc.nc
    with ExitStack() as ctx:
        keep = ctx.enter_context(tc.tile_pool(name="keep", bufs=1))
        psum = ctx.enter_context(tc.psum_pool(name="psum", bufs=1))

        def bank(b):
            return psum.tile([P, BANK], F32, name="bank%d" % b)

        def entries(lst, a, b):
            return lst[:, a // 16 : b // 16]

        tokens = keep.tile([P, J // 16], U16, name="tokens")
        partners = keep.tile([P, J // 16], U16, name="partners")
        x = [keep.tile([P, T], F32, name="x%d" % t) for t in range(PACK)]
        x_rows = xf.rearrange("(p t) c -> p t c", t=PACK)
        nc.sync.dma_start(x[0][:], x_rows[:, 0, :])
        nc.sync.dma_start(partners[:], offs2)
        nc.sync.dma_start(x[1][:], x_rows[:, 1, :])
        nc.sync.dma_start(tokens[:], offs)
        ga_cols = keep.tile([P, PACK], F32, name="ga_cols")
        with nc.allow_non_contiguous_dma(reason="one weight a slot, slots on partitions"):
            nc.sync.dma_start(ga_cols[:], ga.rearrange("o (c p) -> p (o c)", p=P))
        for t in range(2, PACK):
            nc.sync.dma_start(x[t][:], x_rows[:, t, :])
        w_words = keep.tile([P, 2 * N], U8, name="w_words", align_bytes=64)
        nc.sync.dma_start(w_words[:].bitcast(I32), wa_words[0].bitcast(I32))
        w_scales = keep.tile([P, N], U8, name="w_scales", align_bytes=64)
        nc.gpsimd.memset(w_scales[:].bitcast(I32), 0)
        for q in range(4):
            nc.sync.dma_start(w_scales[32 * q : 32 * q + 4, :].bitcast(I32), wa_scales[0, 4 * q : 4 * q + 4, :].bitcast(I32))
        state = [keep.tile([P, T], F32, name="state%d" % b) for b in range(BLOCKS)]
        for b in (1, 0, 2, 3):
            nc.sync.dma_start(state[b][:], old[b * P : (b + 1) * P, :])

        ident = keep.tile([P, P], F32, name="ident")
        make_identity(nc, ident[:])
        placed = [keep.tile([P, T], F32, name="placed%d" % b) for b in range(BLOCKS)]
        for b in range(BLOCKS):
            nc.gpsimd.memset(placed[b][:].bitcast(I32), 0)

        spread = bank(5)
        for c in range(PACK):
            nc.tensor.transpose(spread[:, c * P : (c + 1) * P], ga_cols[:, c : c + 1].to_broadcast([P, P]), ident[:])
        gate = keep.tile([P, J], F32, name="gate")
        gate_twice = keep.tile([P, J], F32, name="gate_twice")
        nc.scalar.activation(gate_twice[:], spread[:], COPY, scale=-2.0)
        nc.scalar.copy(gate[:], spread[:])

        work = keep.tile([P, 6 * HEAD], F32, name="work")
        d_rest = work[:, 0 : PACK * REST].rearrange("p (t c) -> p t c", t=PACK)
        d_head = work[:, 2 * HEAD : 6 * HEAD].rearrange("p (t c) -> p t c", t=PACK)
        g = keep.tile([P, PACK, J], F32, name="g")
        g_last = work[:, HEAD // 2 : 3 * HEAD // 2]

        def fetch(dst, t, a, b):
            nc.vector.tensor_copy(dst, x[t][:].indirect(entries(partners, a, b)))

        def gap_head(t, src):
            nc.vector.tensor_tensor(d_head[:, t, :], x[t][:].indirect(entries(tokens, 0, HEAD)), src, SUB)

        fetch(g[:, 0, :], 0, 0, J)
        fetch(g[:, 1, :], 1, 0, J)
        gap_head(0, g[:, 0, 0:HEAD])
        gap_head(1, g[:, 1, 0:HEAD])
        fetch(g[:, 2, 0:HEAD], 2, 0, HEAD)
        fetch(g[:, 2, HEAD:J], 2, HEAD, J)
        gap_head(2, g[:, 2, 0:HEAD])
        fetch(g_last, 3, 0, HEAD)
        fetch(g[:, 3, HEAD : HEAD + P], 3, HEAD, HEAD + P)
        gap_head(3, g_last)
        fetch(g[:, 3, HEAD + P : J], 3, HEAD + P, J)

        grouped = keep.tile([P, PACK * J], BF16, name="grouped", align_bytes=64)
        codes = keep.tile([P, J], U32, name="codes", align_bytes=64)
        scales = keep.tile([P, J], U8, name="scales", align_bytes=64)

        def interleave(a, b, planes):
            nc.scalar.copy(
                grouped[:, PACK * a : PACK * b].rearrange("p (c i t) -> p c t i", i=4, t=PACK),
                planes.rearrange("p t (c i) -> p c t i", i=4),
            )

        def quantize(a, b):
            nc.vector.quantize_mx(out=codes[:, a:b].bitcast(FP8X4), scales=scales[:, a:b], in_=grouped[:, PACK * a : PACK * b])

        def multiply(acc, blk, a, b):
            nc.tensor.matmul_mx(
                out=acc,
                lhsT=w_words[:, 2 * P * blk : 2 * P * (blk + 1)].bitcast(FP4X4),
                lhsT_scale=w_scales[:, P * blk : P * (blk + 1)],
                rhs=codes[:, a:b].bitcast(FP8X4),
                rhs_scale=scales[:, a:b],
                start=True,
                stop=True,
            )

        def gap_rest(t):
            nc.vector.tensor_tensor(d_rest[:, t, :], x[t][:].indirect(entries(tokens, HEAD, J)), g[:, t, HEAD:J], SUB)

        def scatter(blk, a, b, src):
            factor = gate if blk == 1 else gate_twice
            nc.vector.tensor_tensor(placed[blk][:].indirect(entries(partners, a, b)), src, factor[:, a:b], MULT)

        by_slot = [bank(3), bank(4)]
        weighted = keep.tile([P, 4, 2 * P], F32, name="weighted")
        by_row2 = bank(5)

        def slots_first(c):
            nc.tensor.matmul_mx(
                out=by_slot[c // 2][:, (c % 2) * 2 * P : (c % 2 + 1) * 2 * P],
                lhsT=codes[:, c * P : (c + 1) * P].bitcast(FP8X4),
                lhsT_scale=scales[:, c * P : (c + 1) * P],
                rhs=w_words[:, 2 * P * 2 : 2 * P * 4].bitcast(FP4X4),
                rhs_scale=w_scales[:, P * 2 : P * 4],
                start=True,
                stop=True,
            )

        def weigh(c):
            nc.scalar.activation(weighted[:, c, :], by_slot[c // 2][:, (c % 2) * 2 * P : (c % 2 + 1) * 2 * P], COPY, scale=ga_cols[:, c : c + 1])

        def turn(dst, blk, c):
            nc.tensor.transpose(dst[:, c * P : (c + 1) * P], weighted[:, c, (blk - 2) * P : (blk - 1) * P], ident[:])

        def place(blk, a, b, src):
            nc.vector.tensor_copy(placed[blk][:].indirect(entries(partners, a, b)), src)

        def halve(dst, blk):
            for h in range(2):
                cols = slice(h * BANK, (h + 1) * BANK)
                nc.scalar.activation(dst[:, cols], state[blk][:, cols], COPY, scale=0.5)

        interleave(0, HEAD, d_head)
        gap_rest(0)
        gap_rest(1)
        quantize(0, HEAD)
        acc_head = bank(0)
        for blk in range(2):
            multiply(acc_head[:, blk * HEAD : (blk + 1) * HEAD], blk, 0, HEAD)
        slots_first(0)
        slots_first(1)
        p_head = keep.tile([P, HEAD], F32, name="p_head")
        nc.scalar.copy(p_head[:], acc_head[:, 0:HEAD])
        gap_rest(2)
        gap_rest(3)

        interleave(HEAD, J, d_rest)
        scatter(0, 0, HEAD, p_head[:])
        quantize(HEAD, J)
        acc_rest = bank(1)
        for blk in range(2):
            multiply(acc_rest[:, blk * REST : (blk + 1) * REST], blk, HEAD, J)
        slots_first(2)
        slots_first(3)
        nc.scalar.copy(work[:, 0:HEAD], acc_head[:, HEAD : 2 * HEAD])
        scatter(1, 0, HEAD, work[:, 0:HEAD])
        p_rest = keep.tile([P, BLOCKS, J], F32, name="p_rest")
        for blk in range(2):
            nc.scalar.copy(p_rest[:, blk, HEAD:J], acc_rest[:, blk * REST : (blk + 1) * REST])
        for c in range(4):
            weigh(c)
        by_row3 = bank(2)
        for c in range(4):
            turn(by_row2, 2, c)
        for c in range(4):
            turn(by_row3, 3, c)
        nc.scalar.copy(p_rest[:, 2, :], by_row2[:])
        nc.scalar.copy(p_rest[:, 3, :], by_row3[:])
        half1 = keep.tile([P, T], F32, name="half1")
        halve(half1, 1)
        half2 = work[:, BANK : BANK + T]
        halve(half2, 2)
        result = [keep.tile([P, T], F32, name="result%d" % b) for b in range(BLOCKS)]

        def on_gpsimd(blk, half):
            for h in range(2):
                cols = slice(h * BANK, (h + 1) * BANK)
                nc.gpsimd.tensor_tensor(result[blk][:, cols], half[:, cols], placed[blk][:, cols], SUB)
                nc.sync.dma_start(out[blk * P : (blk + 1) * P, cols], result[blk][:, cols])

        sums = [bank(5), bank(2)]
        for h in range(2):
            for c in range(4):
                col = h * BANK + c * P
                nc.tensor.matmul(sums[h][:, c * P : (c + 1) * P], state[0][:, col : col + P], ident[:], start=(c == 0), stop=False, is_transpose=True)
        scatter(0, HEAD, J, p_rest[:, 0, HEAD:J])
        turned = keep.tile([P, T], F32, name="turned")
        for h in range(2):
            cols = slice(h * BANK, (h + 1) * BANK)
            for c in range(4):
                col = h * BANK + c * P
                nc.tensor.matmul(sums[h][:, c * P : (c + 1) * P], placed[0][:, col : col + P], ident[:], start=False, stop=(c == 3), is_transpose=True)
            nc.scalar.activation(turned[:, cols], sums[h][:], COPY, scale=0.5)
        for h in range(2):
            cols = slice(h * BANK, (h + 1) * BANK)
            back = bank(3 + h)
            for c in range(4):
                col = h * BANK + c * P
                nc.tensor.transpose(back[:, c * P : (c + 1) * P], turned[:, col : col + P], ident[:])
            nc.scalar.copy(result[0][:, cols], back[:])
            nc.scalar.dma_start(out[0:P, cols], result[0][:, cols])

        scatter(1, HEAD, J, p_rest[:, 1, HEAD:J])
        on_gpsimd(1, half1)
        place(2, 0, J, p_rest[:, 2, :])
        on_gpsimd(2, half2)
        place(3, 0, J, p_rest[:, 3, :])
        for cols in (slice(0, 320), slice(320, 672), slice(672, T)):
            nc.vector.scalar_tensor_tensor(result[3][:, cols], state[3][:, cols], 0.5, placed[3][:, cols], MULT, SUB)
            nc.sync.dma_start(out[3 * P : 4 * P, cols], result[3][:, cols])
